import numpy as np
import ml_dtypes


def mxq(x, axis, fmt="e4m3"):
    dtype, down = {"e4m3": (ml_dtypes.float8_e4m3fn, 7), "e5m2": (ml_dtypes.float8_e5m2, 14)}[fmt]
    v = np.moveaxis(np.asarray(x, np.float32).astype(ml_dtypes.bfloat16).astype(np.float64), axis, -1)
    blocks = v.reshape(v.shape[:-1] + (-1, 32))
    amax = np.abs(blocks).max(-1, keepdims=True)
    byte = np.maximum(np.where(amax > 0, np.frexp(amax)[1] - 1 + 127, 0) - down, 1)
    scale = np.exp2(byte - 127.0)
    codes = (blocks / scale).astype(np.float32).astype(dtype).astype(np.float64)
    return np.moveaxis((codes * scale).reshape(v.shape), -1, axis)


WIDE = False


def mx_kscale(k):
    if not WIDE:
        return np.ones(k)
    levels = np.array([10, -10, 5, -5, 0])
    if k % 512:
        return np.exp2(np.random.permutation(np.resize(levels, k // 32))).repeat(32)
    a = np.empty((k // 512, 16))
    for p in range(k // 512):
        a[p, :8] = np.random.permutation(np.resize(levels, 8))
        for g in range(8):
            far = levels[np.abs(levels - a[p, g]) >= 10]
            a[p, g + 8] = far[np.random.randint(len(far))]
    return np.exp2(a.ravel()).repeat(32)


def f64(x):
    return np.asarray(x).astype(np.float64)


def striped(idx):
    return np.tile(idx.reshape(-1, 16).T, (8, 1)).astype(np.uint16)


def unstriped(offs):
    return offs[:16].T.reshape(-1).astype(np.int64)


def pack_weight(w):
    k, n = w.shape
    w = f64(np.asarray(w, np.float32).astype(ml_dtypes.bfloat16)).reshape(k // 32, 32, n)
    amax = np.abs(w).max(1)
    byte = np.clip(np.where(amax > 0, np.frexp(amax)[1] - 1 + 127 - 7, 1), 1, 254)
    scaled = (w * np.exp2(127.0 - byte)[:, None, :]).reshape(k, n).astype(np.float32)
    words = np.ascontiguousarray(scaled.reshape(k // 512, 128, 4, n).transpose(0, 1, 3, 2)).astype(ml_dtypes.float8_e4m3fn).view(np.uint8)
    return words, np.ascontiguousarray(byte.astype(np.uint8).reshape(k // 512, 16, n))


def unpack_weight(words, scales):
    g, p, n, _ = words.shape
    vals = np.ascontiguousarray(words).view(ml_dtypes.float8_e4m3fn).astype(np.float64) * np.repeat(np.exp2(scales.astype(np.float64) - 127.0), 8, axis=1)[..., None]
    return vals.transpose(0, 1, 3, 2).reshape(g * 512, n)


K, T, S, V, D, U = 512, 1024, 512, 512, 8, 1024


def setup_inputs():
    n = np.random.standard_normal
    s = mx_kscale(K)[:, None]
    packed_xT = pack_weight(n((K, T)) * s)
    return {
        "x_words": packed_xT[0],
        "x_scales": packed_xT[1],
        "hT": (n((K, V)) / np.sqrt(K) / s).astype(np.float32),
        "offs": striped(np.random.permutation(T)[:S]),
        "win": striped(np.random.permutation(np.concatenate([np.arange(S), np.random.randint(0, S, U - S)]))),
        "lose": striped(np.random.permutation(np.concatenate([np.arange(S), np.random.randint(0, S, U - S)]))),
    }


def reference(x_words, x_scales, hT, offs, win, lose):
    hTq = mxq(f64(hT), 0, "e4m3")
    xq = unpack_weight(x_words, x_scales)[:, unstriped(offs)]
    y = hTq.T @ xq
    ex = np.exp(y)
    ls = np.log(ex.sum(axis=1, keepdims=True))
    lp = y - ls
    lw = lp[:, unstriped(win)]
    mw = lw.reshape(len(lw), -1, D).mean(axis=2)
    ll = lp[:, unstriped(lose)]
    ml = ll.reshape(len(ll), -1, D).mean(axis=2)
    gap = 2.5 * (mw - ml)
    return np.log(np.exp(-1.0 * gap + 0.7) + 1.0) - (0.3 * mw)

@@ -1,0 +1,205 @@
+from contextlib import ExitStack
+
+import concourse.mybir as mybir
+from concourse.masks import make_identity
+
+K, T, S, V, D, U = 512, 1024, 512, 512, 8, 1024
+G = U // D
+FLOPS = 2 * K * V * S
+
+F32 = mybir.dt.float32
+BF16 = mybir.dt.bfloat16
+I32 = mybir.dt.int32
+U32 = mybir.dt.uint32
+U16 = mybir.dt.uint16
+U8 = mybir.dt.uint8
+FP8X4 = mybir.dt.float8_e4m3fn_x4
+ALU = mybir.AluOpType
+ACT = mybir.ActivationFunctionType
+
+P = 128
+PACK = 4
+BLOCKS = V // P
+SCALAR_BLOCKS = (0, 1)
+VECTOR_BLOCKS = (2, 3)
+PIECE = 512
+SCALAR_WINDOW = 2048
+VECTOR_WINDOW = 1024
+BETA, MARGIN, NLL = 2.5, 0.7, 0.3
+CAP = 30.0
+
+
+def tile_picked_ysimpo_simpo_p_kernel(tc, x_words, x_scales, hT, offs, win, lose, out):
+    nc = tc.nc
+    with ExitStack() as ctx:
+        keep = ctx.enter_context(tc.tile_pool(name="keep", bufs=1))
+        psum = ctx.enter_context(tc.psum_pool(name="psum", bufs=1))
+
+        offs_t = keep.tile([P, S // 16], U16, name="offs_t")
+        win_t = keep.tile([P, U // 16], U16, name="win_t")
+        lose_t = keep.tile([P, U // 16], U16, name="lose_t")
+        words = keep.tile([P, T], I32, name="words", align_bytes=64)
+        scales = keep.tile([P, T], U8, name="scales", align_bytes=64)
+        h_raw = [keep.tile([P, PACK, width], F32, name=f"h_raw{i}") for i, width in enumerate((P, P, 2 * P))]
+        h_rows = hT.rearrange("(p j) t -> p j t", j=PACK)
+
+        nc.gpsimd.memset(scales[:].bitcast(I32), 0)
+        nc.sync.dma_start(offs_t[:], offs)
+        nc.sync.dma_start(h_raw[0][:], h_rows[:, :, 0:P])
+        for q in range(4):
+            nc.scalar.dma_start(scales[32 * q : 32 * q + 4, :].bitcast(I32), x_scales[0, 4 * q : 4 * q + 4, :].bitcast(I32))
+        nc.sync.dma_start(words[:], x_words[0].rearrange("p n t -> p (n t)").bitcast(I32))
+        nc.sync.dma_start(h_raw[1][:], h_rows[:, :, P : 2 * P])
+        nc.sync.dma_start(h_raw[2][:], h_rows[:, :, 2 * P : V])
+        nc.sync.dma_start(win_t[:], win)
+        nc.sync.dma_start(lose_t[:], lose)
+        h_block = [h_raw[0][:], h_raw[1][:], h_raw[2][:, :, 0:P], h_raw[2][:, :, P : 2 * P]]
+
+        ident = keep.tile([P, P], F32, name="ident")
+        make_identity(nc, ident[:])
+
+        row_const = keep.tile([P, BLOCKS], F32, name="row_const")
+        nc.vector.memset(row_const[:, 0:2], -1.0)
+        one = keep.tile([P, 1], F32, name="one")
+        nc.vector.memset(one[:], 1.0)
+        warm = keep.tile([P, 1], F32, name="warm")
+        nc.scalar.activation(warm[:], one[:], ACT.Ln)
+
+        x_codes = keep.tile([P, S], U32, name="x_codes", align_bytes=64)
+        x_bytes = keep.tile([P, S], U8, name="x_bytes", align_bytes=64)
+        nc.vector.tensor_copy(x_bytes[:], scales[:].indirect(offs_t[:]))
+        nc.vector.tensor_copy(x_codes[:], words[:].bitcast(U32).indirect(offs_t[:]))
+
+        logits = []
+        for b in range(BLOCKS):
+            grouped = keep.tile([P, P, PACK], BF16, name=f"grouped{b}", align_bytes=64)
+            src = h_block[b]
+            nc.scalar.copy(
+                grouped[:].rearrange("p (c i) j -> p c j i", i=4),
+                src.rearrange("p j (c i) -> p c j i", i=4),
+            )
+            h_codes = keep.tile([P, P], U32, name=f"h_codes{b}", align_bytes=64)
+            h_bytes = keep.tile([P, P], U8, name=f"h_bytes{b}", align_bytes=64)
+            nc.vector.quantize_mx(out=h_codes[:].bitcast(FP8X4), scales=h_bytes[:], in_=grouped[:].rearrange("p t j -> p (t j)"))
+            y = psum.tile([P, S], F32, name=f"y{b}", tag=f"bank{b}")
+            nc.tensor.matmul_mx(
+                out=y[:], lhsT=h_codes[:].bitcast(FP8X4), lhsT_scale=h_bytes[:],
+                rhs=x_codes[:].bitcast(FP8X4), rhs_scale=x_bytes[:], start=True, stop=True,
+            )
+            logits.append(y)
+
+        picked = {}
+        for b in range(BLOCKS):
+            for name in ("win", "lose"):
+                picked[b, name] = keep.tile([P, U], F32, name=f"picked_{name}{b}")
+        top = {0: picked[0, "win"][:, 0:1], 1: picked[0, "win"][:, 1:2], 2: row_const[:, 2:3], 3: row_const[:, 3:4]}
+        neg_top = keep.tile([P, BLOCKS], F32, name="neg_top")
+
+        lifted, window = {}, {}
+
+        def open_block(b):
+            lifted[b] = keep.tile([P, S if b in SCALAR_BLOCKS else VECTOR_WINDOW], F32, name=f"lifted{b}")
+            nc.vector.tensor_scalar(lifted[b][:, 0:S], logits[b][:], 1.0, None, ALU.add, ALU.max, accum_out=top[b])
+            if b in SCALAR_BLOCKS:
+                window[b] = keep.tile([P, SCALAR_WINDOW], F32, name=f"log_window{b}")
+                nc.scalar.activation(window[b][:, 0:S], logits[b][:], ACT.Ln, bias=top[b], scale=-1.0)
+            else:
+                window[b] = lifted[b]
+
+        open_block(0)
+        open_block(1)
+        nc.vector.tensor_scalar(neg_top[:, 0:2], picked[0, "win"][:, 0:2], -1.0, None, ALU.mult)
+        open_block(2)
+        row_part = keep.tile([P, BLOCKS], F32, name="row_part")
+
+        lists = {"win": win_t, "lose": lose_t}
+        order = [(2, "win"), (0, "win"), (2, "lose"), (0, "lose"), (3, "win"), (1, "win"), (3, "lose"), (1, "lose")]
+        bank_of = [4, 5, 5, 6, 6, 7, 7, 0]
+        banks = {}
+        sums = {}
+
+        def gather(b, name):
+            for h in range(U // PIECE):
+                dst = picked[b, name][:, h * PIECE : (h + 1) * PIECE]
+                src = window[b][:].indirect(lists[name][:, h * (PIECE // 16) : (h + 1) * (PIECE // 16)])
+                if b in SCALAR_BLOCKS:
+                    nc.scalar.activation(dst, src, ACT.Exp)
+                else:
+                    nc.vector.tensor_copy(dst, src)
+
+        def add_up(n, b, name):
+            bank = bank_of[n]
+            if bank not in banks:
+                banks[bank] = psum.tile([P, 2, P], F32, name=f"sums{bank}", tag=f"bank{bank}")
+            acc = banks[bank][:, n % 2, :]
+            groups = picked[b, name][:].rearrange("p (g d) -> p g d", d=D)
+            if n < 4:
+                terms = [groups[:, :, d] for d in range(D)]
+            else:
+                half = keep.tile([P, D // 2, G], F32, name=f"half_{name}{b}")
+                nc.vector.tensor_tensor(half[:].rearrange("p d g -> p g d"), groups[:, :, 0 : D // 2], groups[:, :, D // 2 : D], ALU.add)
+                terms = [half[:, d, :] for d in range(D // 2)]
+            for i, term in enumerate(terms):
+                nc.tensor.matmul(acc, term, ident[:], start=(i == 0), stop=(i == len(terms) - 1), is_transpose=True)
+            sums[b, name] = acc
+
+        wanted = keep.tile([P, BLOCKS, P], F32, name="wanted")
+        arg = keep.tile([P, BLOCKS, P], F32, name="arg")
+        capped = keep.tile([P, BLOCKS, P], F32, name="capped")
+        excess = keep.tile([P, BLOCKS, P], F32, name="excess")
+        linear = keep.tile([P, BLOCKS, P], F32, name="linear")
+        ln_in = keep.tile([P, V + BLOCKS], F32, name="ln_in")
+        ln_out = keep.tile([P, V + BLOCKS], F32, name="ln_out")
+        slope = BETA / D
+
+        def sign(b):
+            return 1.0 if b in SCALAR_BLOCKS else -1.0
+
+        def take_wanted(b):
+            nc.vector.tensor_scalar(wanted[:, b, :], sums[b, "win"], sign(b) * slope, None, ALU.mult)
+
+        def take_gap(b):
+            nc.vector.scalar_tensor_tensor(arg[:, b, :], sums[b, "lose"], -sign(b) * slope, wanted[:, b, :], ALU.mult, ALU.add)
+            nc.vector.tensor_scalar(capped[:, b, :], arg[:, b, :], MARGIN, CAP, ALU.add, ALU.min)
+            nc.scalar.activation(ln_in[:, b * P : (b + 1) * P], capped[:, b, :], ACT.Exp)
+
+        def take_linear(b):
+            nc.vector.tensor_scalar(excess[:, b, :], arg[:, b, :], MARGIN - CAP, 0.0, ALU.add, ALU.max)
+            nc.vector.scalar_tensor_tensor(linear[:, b, :], wanted[:, b, :], NLL / BETA, excess[:, b, :], ALU.mult, ALU.add)
+
+        for n in range(0, 8, 2):
+            gather(*order[n])
+            gather(*order[n + 1])
+            add_up(n, *order[n])
+            add_up(n + 1, *order[n + 1])
+            if n == 0:
+                open_block(3)
+                nc.vector.tensor_scalar(neg_top[:, 2:4], row_const[:, 2:4], -1.0, None, ALU.mult)
+                nc.vector.tensor_scalar(row_part[:], row_const[:], NLL, None, ALU.mult)
+        row_sum = keep.tile([P, BLOCKS], F32, name="row_sum")
+        exps = keep.tile([P, BLOCKS, S], F32, name="exps")
+        for b in range(BLOCKS):
+            nc.scalar.activation(exps[:, b, :], lifted[b][:, 0:S], ACT.Exp, bias=neg_top[:, b : b + 1], accum_out=row_sum[:, b : b + 1])
+        nc.vector.tensor_scalar(ln_in[:, V : V + BLOCKS], row_sum[:], -1.0, None, ALU.add)
+        for b in (2, 0, 3, 1):
+            take_wanted(b)
+            take_gap(b)
+        for b in range(BLOCKS):
+            take_linear(b)
+
+        nc.scalar.activation(ln_out[:], ln_in[:], ACT.Ln, bias=one[:])
+        row_bias = keep.tile([P, BLOCKS], F32, name="row_bias")
+        nc.vector.scalar_tensor_tensor(row_bias[:], ln_out[:, V : V + BLOCKS], NLL, row_part[:], ALU.mult, ALU.add)
+
+        result = keep.tile([P, BLOCKS, G], F32, name="result")
+        back = {}
+        for b in range(BLOCKS):
+            back[b] = psum.tile([P, G], F32, name=f"back{b}", tag=f"bank{b + 1}")
+            nc.tensor.matmul(back[b][:], linear[:, b, :], ident[:], start=True, stop=False, is_transpose=True)
+        for b in range(BLOCKS):
+            nc.tensor.matmul(back[b][:], ln_out[:, b * P : (b + 1) * P], ident[:], start=False, stop=True, is_transpose=True)
+            if b % 2 == 0:
+                nc.vector.tensor_scalar(result[:, b, :], back[b][:], row_bias[:, b : b + 1], None, ALU.add)
+            else:
+                nc.scalar.activation(result[:, b, :], back[b][:], ACT.Identity, bias=row_bias[:, b : b + 1])
+            nc.sync.dma_start(out[b * P : (b + 1) * P, :], result[:, b, :])

@@ -24,7 +24,7 @@ SCALAR_BLOCKS = (0, 1)
 VECTOR_BLOCKS = (2, 3)
 PIECE = 512
 SCALAR_WINDOW = 2048
-VECTOR_WINDOW = 1024
+VECTOR_WINDOW = 2048
 BETA, MARGIN, NLL = 2.5, 0.7, 0.3
 CAP = 30.0
 
@@ -40,59 +40,66 @@ def tile_picked_ysimpo_simpo_p_kernel(tc, x_words, x_scales, hT, offs, win, lose
         lose_t = keep.tile([P, U // 16], U16, name="lose_t")
         words = keep.tile([P, T], I32, name="words", align_bytes=64)
         scales = keep.tile([P, T], U8, name="scales", align_bytes=64)
-        h_raw = [keep.tile([P, PACK, width], F32, name=f"h_raw{i}") for i, width in enumerate((P, P, 2 * P))]
+        h_raw = [keep.tile([P, PACK, P], F32, name=f"h_raw{b}", tag=f"h_raw{b}") for b in range(BLOCKS)]
         h_rows = hT.rearrange("(p j) t -> p j t", j=PACK)
 
-        nc.gpsimd.memset(scales[:].bitcast(I32), 0)
         nc.sync.dma_start(offs_t[:], offs)
-        nc.sync.dma_start(h_raw[0][:], h_rows[:, :, 0:P])
         for q in range(4):
-            nc.scalar.dma_start(scales[32 * q : 32 * q + 4, :].bitcast(I32), x_scales[0, 4 * q : 4 * q + 4, :].bitcast(I32))
+            rows = x_scales[0, 4 * q : 4 * q + 4, :].bitcast(I32)
+            queue = nc.sync if q == 0 else nc.scalar
+            queue.dma_start(scales[32 * q : 32 * q + 32, :].bitcast(I32), rows.unsqueeze(0).to_broadcast([8, 4, T // 4]))
+        nc.sync.dma_start(h_raw[0][:], h_rows[:, :, 0:P])
         nc.sync.dma_start(words[:], x_words[0].rearrange("p n t -> p (n t)").bitcast(I32))
-        nc.sync.dma_start(h_raw[1][:], h_rows[:, :, P : 2 * P])
-        nc.sync.dma_start(h_raw[2][:], h_rows[:, :, 2 * P : V])
+        for b in range(1, BLOCKS):
+            nc.sync.dma_start(h_raw[b][:], h_rows[:, :, b * P : (b + 1) * P])
         nc.sync.dma_start(win_t[:], win)
         nc.sync.dma_start(lose_t[:], lose)
-        h_block = [h_raw[0][:], h_raw[1][:], h_raw[2][:, :, 0:P], h_raw[2][:, :, P : 2 * P]]
+        h_block = [h_raw[b][:] for b in range(BLOCKS)]
 
+        ones = keep.tile([P, 2], F32, name="ones")
+        nc.gpsimd.memset(ones[:], 1.0)
+        one = ones[:, 0:1]
+        margin = keep.tile([P, 1], F32, name="margin")
+        nc.gpsimd.tensor_scalar(margin[:], one, MARGIN, 0.0, ALU.mult, ALU.add)
+        row_part = keep.tile([P, BLOCKS], F32, name="row_part")
+        nc.gpsimd.tensor_scalar(row_part[:, 0:2], ones[:], -NLL, 0.0, ALU.mult, ALU.add)
         ident = keep.tile([P, P], F32, name="ident")
         make_identity(nc, ident[:])
 
-        row_const = keep.tile([P, BLOCKS], F32, name="row_const")
-        nc.vector.memset(row_const[:, 0:2], -1.0)
-        one = keep.tile([P, 1], F32, name="one")
-        nc.vector.memset(one[:], 1.0)
         warm = keep.tile([P, 1], F32, name="warm")
-        nc.scalar.activation(warm[:], one[:], ACT.Ln)
+        nc.scalar.activation(warm[:], one, ACT.Ln)
 
         x_codes = keep.tile([P, S], U32, name="x_codes", align_bytes=64)
         x_bytes = keep.tile([P, S], U8, name="x_bytes", align_bytes=64)
         nc.vector.tensor_copy(x_bytes[:], scales[:].indirect(offs_t[:]))
         nc.vector.tensor_copy(x_codes[:], words[:].bitcast(U32).indirect(offs_t[:]))
 
-        logits = []
+        logits = {}
+
+        interleaved = []
         for b in range(BLOCKS):
             grouped = keep.tile([P, P, PACK], BF16, name=f"grouped{b}", align_bytes=64)
-            src = h_block[b]
             nc.scalar.copy(
                 grouped[:].rearrange("p (c i) j -> p c j i", i=4),
-                src.rearrange("p j (c i) -> p c j i", i=4),
+                h_block[b].rearrange("p j (c i) -> p c j i", i=4),
             )
-            h_codes = keep.tile([P, P], U32, name=f"h_codes{b}", align_bytes=64)
-            h_bytes = keep.tile([P, P], U8, name=f"h_bytes{b}", align_bytes=64)
+            interleaved.append(grouped)
+
+        def multiply(b):
+            grouped = interleaved[b]
+            h_codes = keep.tile([P, P], U32, name=f"h_codes{b}", tag="h_codes", bufs=3, align_bytes=64)
+            h_bytes = keep.tile([P, P], U8, name=f"h_bytes{b}", tag="h_bytes", bufs=3, align_bytes=64)
             nc.vector.quantize_mx(out=h_codes[:].bitcast(FP8X4), scales=h_bytes[:], in_=grouped[:].rearrange("p t j -> p (t j)"))
-            y = psum.tile([P, S], F32, name=f"y{b}", tag=f"bank{b}")
+            logits[b] = psum.tile([P, S], F32, name=f"y{b}", tag=f"bank{b}")
             nc.tensor.matmul_mx(
-                out=y[:], lhsT=h_codes[:].bitcast(FP8X4), lhsT_scale=h_bytes[:],
+                out=logits[b][:], lhsT=h_codes[:].bitcast(FP8X4), lhsT_scale=h_bytes[:],
                 rhs=x_codes[:].bitcast(FP8X4), rhs_scale=x_bytes[:], start=True, stop=True,
             )
-            logits.append(y)
 
-        picked = {}
-        for b in range(BLOCKS):
-            for name in ("win", "lose"):
-                picked[b, name] = keep.tile([P, U], F32, name=f"picked_{name}{b}")
-        top = {0: picked[0, "win"][:, 0:1], 1: picked[0, "win"][:, 1:2], 2: row_const[:, 2:3], 3: row_const[:, 3:4]}
+        top0 = keep.tile([P, 1], F32, name="top0")
+        top1 = keep.tile([P, 1], F32, name="top1", tag="first_picked")
+        tops = keep.tile([P, 2], F32, name="tops")
+        top = {0: top0[:], 1: top1[:], 2: tops[:, 0:1], 3: tops[:, 1:2]}
         neg_top = keep.tile([P, BLOCKS], F32, name="neg_top")
 
         lifted, window = {}, {}
@@ -101,105 +108,153 @@ def tile_picked_ysimpo_simpo_p_kernel(tc, x_words, x_scales, hT, offs, win, lose
             lifted[b] = keep.tile([P, S if b in SCALAR_BLOCKS else VECTOR_WINDOW], F32, name=f"lifted{b}")
             nc.vector.tensor_scalar(lifted[b][:, 0:S], logits[b][:], 1.0, None, ALU.add, ALU.max, accum_out=top[b])
             if b in SCALAR_BLOCKS:
-                window[b] = keep.tile([P, SCALAR_WINDOW], F32, name=f"log_window{b}")
+                window[b] = keep.tile([P, SCALAR_WINDOW], F32, name=f"log_window{b}", tag=f"h_raw{3 - b}")
                 nc.scalar.activation(window[b][:, 0:S], logits[b][:], ACT.Ln, bias=top[b], scale=-1.0)
+                nc.scalar.mul(neg_top[:, b : b + 1], top[b], -1.0)
             else:
                 window[b] = lifted[b]
 
+        multiply(0)
+        multiply(1)
+        multiply(2)
         open_block(0)
         open_block(1)
-        nc.vector.tensor_scalar(neg_top[:, 0:2], picked[0, "win"][:, 0:2], -1.0, None, ALU.mult)
         open_block(2)
-        row_part = keep.tile([P, BLOCKS], F32, name="row_part")
+        multiply(3)
 
+        picked = {}
+        for b in range(BLOCKS):
+            both = keep.tile([P, 2 * U], F32, name=f"picked{b}", tag="first_picked" if b == 0 else f"picked{b}")
+            picked[b, "win"], picked[b, "lose"] = both[:, 0:U], both[:, U : 2 * U]
         lists = {"win": win_t, "lose": lose_t}
-        order = [(2, "win"), (0, "win"), (2, "lose"), (0, "lose"), (3, "win"), (1, "win"), (3, "lose"), (1, "lose")]
-        bank_of = [4, 5, 5, 6, 6, 7, 7, 0]
-        banks = {}
-        sums = {}
-
-        def gather(b, name):
-            for h in range(U // PIECE):
-                dst = picked[b, name][:, h * PIECE : (h + 1) * PIECE]
-                src = window[b][:].indirect(lists[name][:, h * (PIECE // 16) : (h + 1) * (PIECE // 16)])
-                if b in SCALAR_BLOCKS:
-                    nc.scalar.activation(dst, src, ACT.Exp)
-                else:
-                    nc.vector.tensor_copy(dst, src)
-
-        def add_up(n, b, name):
-            bank = bank_of[n]
-            if bank not in banks:
-                banks[bank] = psum.tile([P, 2, P], F32, name=f"sums{bank}", tag=f"bank{bank}")
-            acc = banks[bank][:, n % 2, :]
-            groups = picked[b, name][:].rearrange("p (g d) -> p g d", d=D)
-            if n < 4:
-                terms = [groups[:, :, d] for d in range(D)]
-            else:
-                half = keep.tile([P, D // 2, G], F32, name=f"half_{name}{b}")
-                nc.vector.tensor_tensor(half[:].rearrange("p d g -> p g d"), groups[:, :, 0 : D // 2], groups[:, :, D // 2 : D], ALU.add)
-                terms = [half[:, d, :] for d in range(D // 2)]
-            for i, term in enumerate(terms):
-                nc.tensor.matmul(acc, term, ident[:], start=(i == 0), stop=(i == len(terms) - 1), is_transpose=True)
-            sums[b, name] = acc
-
-        wanted = keep.tile([P, BLOCKS, P], F32, name="wanted")
-        arg = keep.tile([P, BLOCKS, P], F32, name="arg")
-        capped = keep.tile([P, BLOCKS, P], F32, name="capped")
-        excess = keep.tile([P, BLOCKS, P], F32, name="excess")
-        linear = keep.tile([P, BLOCKS, P], F32, name="linear")
-        ln_in = keep.tile([P, V + BLOCKS], F32, name="ln_in")
-        ln_out = keep.tile([P, V + BLOCKS], F32, name="ln_out")
+        pieces = U // PIECE
+        per_piece = PIECE // D
         slope = BETA / D
 
-        def sign(b):
-            return 1.0 if b in SCALAR_BLOCKS else -1.0
+        def piece(b, name, h):
+            return picked[b, name][:, h * PIECE : (h + 1) * PIECE]
 
-        def take_wanted(b):
-            nc.vector.tensor_scalar(wanted[:, b, :], sums[b, "win"], sign(b) * slope, None, ALU.mult)
+        def looked_up(b, name, first, count):
+            return window[b][:].indirect(lists[name][:, first // 16 : (first + count) // 16])
 
-        def take_gap(b):
-            nc.vector.scalar_tensor_tensor(arg[:, b, :], sums[b, "lose"], -sign(b) * slope, wanted[:, b, :], ALU.mult, ALU.add)
-            nc.vector.tensor_scalar(capped[:, b, :], arg[:, b, :], MARGIN, CAP, ALU.add, ALU.min)
-            nc.scalar.activation(ln_in[:, b * P : (b + 1) * P], capped[:, b, :], ACT.Exp)
+        def scalar_gather(b, name):
+            for h in range(pieces):
+                nc.scalar.activation(piece(b, name, h), looked_up(b, name, h * PIECE, PIECE), ACT.Exp)
 
-        def take_linear(b):
-            nc.vector.tensor_scalar(excess[:, b, :], arg[:, b, :], MARGIN - CAP, 0.0, ALU.add, ALU.max)
-            nc.vector.scalar_tensor_tensor(linear[:, b, :], wanted[:, b, :], NLL / BETA, excess[:, b, :], ALU.mult, ALU.add)
+        def vector_win(b):
+            nc.vector.tensor_copy(picked[b, "win"], looked_up(b, "win", 0, U))
 
-        for n in range(0, 8, 2):
-            gather(*order[n])
-            gather(*order[n + 1])
-            add_up(n, *order[n])
-            add_up(n + 1, *order[n + 1])
-            if n == 0:
-                open_block(3)
-                nc.vector.tensor_scalar(neg_top[:, 2:4], row_const[:, 2:4], -1.0, None, ALU.mult)
-                nc.vector.tensor_scalar(row_part[:], row_const[:], NLL, None, ALU.mult)
-        row_sum = keep.tile([P, BLOCKS], F32, name="row_sum")
-        exps = keep.tile([P, BLOCKS, S], F32, name="exps")
-        for b in range(BLOCKS):
-            nc.scalar.activation(exps[:, b, :], lifted[b][:, 0:S], ACT.Exp, bias=neg_top[:, b : b + 1], accum_out=row_sum[:, b : b + 1])
-        nc.vector.tensor_scalar(ln_in[:, V : V + BLOCKS], row_sum[:], -1.0, None, ALU.add)
-        for b in (2, 0, 3, 1):
-            take_wanted(b)
-            take_gap(b)
-        for b in range(BLOCKS):
-            take_linear(b)
+        def vector_lose(b, first, count, dst):
+            nc.vector.tensor_tensor(dst, looked_up(b, "lose", first, count), picked[b, "win"][:, first : first + count], ALU.subtract)
 
-        nc.scalar.activation(ln_out[:], ln_in[:], ACT.Ln, bias=one[:])
-        row_bias = keep.tile([P, BLOCKS], F32, name="row_bias")
-        nc.vector.scalar_tensor_tensor(row_bias[:], ln_out[:, V : V + BLOCKS], NLL, row_part[:], ALU.mult, ALU.add)
+        def add_terms(acc, terms, opens=True, closes=True):
+            for i, term in enumerate(terms):
+                first, final = opens and i == 0, closes and i == len(terms) - 1
+                nc.tensor.matmul(acc, term, ident[:], start=first, stop=final, is_transpose=True)
 
-        result = keep.tile([P, BLOCKS, G], F32, name="result")
-        back = {}
-        for b in range(BLOCKS):
-            back[b] = psum.tile([P, G], F32, name=f"back{b}", tag=f"bank{b + 1}")
-            nc.tensor.matmul(back[b][:], linear[:, b, :], ident[:], start=True, stop=False, is_transpose=True)
-        for b in range(BLOCKS):
-            nc.tensor.matmul(back[b][:], ln_out[:, b * P : (b + 1) * P], ident[:], start=False, stop=True, is_transpose=True)
-            if b % 2 == 0:
-                nc.vector.tensor_scalar(result[:, b, :], back[b][:], row_bias[:, b : b + 1], None, ALU.add)
+        def eighths(b, name):
+            groups = picked[b, name].rearrange("p (g d) -> p g d", d=D)
+            return [groups[:, :, d] for d in range(D)]
+
+        halves = {}
+
+        def fold(b, name, first, src, negate):
+            if (b, name) not in halves:
+                slot = "half_late" if (b, name) in ((1, "lose"), (3, "win")) else f"half_{name}{b}"
+                halves[b, name] = keep.tile([P, D // 2, G], F32, name=f"half_{name}{b}", tag=slot)
+            groups = src.rearrange("p (g d) -> p g d", d=D)
+            dst = halves[b, name][:, :, first : first + groups.shape[1]].rearrange("p d g -> p g d")
+            if negate:
+                nc.vector.scalar_tensor_tensor(dst, groups[:, :, 0 : D // 2], -1.0, groups[:, :, D // 2 : D], ALU.mult, ALU.subtract)
             else:
-                nc.scalar.activation(result[:, b, :], back[b][:], ACT.Identity, bias=row_bias[:, b : b + 1])
+                nc.vector.tensor_tensor(dst, groups[:, :, 0 : D // 2], groups[:, :, D // 2 : D], ALU.add)
+
+        def quarters(b, name):
+            return [halves[b, name][:, d, :] for d in range(D // 2)]
+
+        bank4 = psum.tile([P, P], F32, name="sum_a", tag="bank4")
+        bank5 = psum.tile([P, 2, P], F32, name="sum_b", tag="bank5")
+        bank6 = psum.tile([P, P], F32, name="sum_c", tag="bank6")
+        bank7 = psum.tile([P, P], F32, name="sum_d", tag="bank7")
+        win_sum = {2: bank4[:], 0: bank5[:, 0, :]}
+        lose_sum0 = bank6[:]
+        gap_sum = {2: bank5[:, 1, :], 3: bank7[:]}
+
+        vector_win(2)
+        scalar_gather(0, "win")
+        add_terms(win_sum[2], eighths(2, "win"))
+        add_terms(win_sum[0], eighths(0, "win"))
+        vector_lose(2, 0, U, picked[2, "lose"])
+        scalar_gather(0, "lose")
+        add_terms(gap_sum[2], eighths(2, "lose"))
+        add_terms(lose_sum0, eighths(0, "lose"))
+        open_block(3)
+        nc.gpsimd.tensor_scalar(neg_top[:, 2:4], tops[:], -1.0, 0.0, ALU.mult, ALU.add)
+        nc.gpsimd.tensor_scalar(row_part[:, 2:4], tops[:], NLL, 0.0, ALU.mult, ALU.add)
+
+        vector_win(3)
+        scalar_gather(1, "win")
+        vector_lose(3, 0, PIECE, piece(3, "lose", 0))
+        scalar_gather(1, "lose")
+        fold(1, "win", 0, picked[1, "win"], False)
+        bank0 = psum.tile([P, 3, P], F32, name="sum_e", tag="bank0")
+        gap_sum[1], win_sum[1], win_sum[3] = bank0[:, 0, :], bank0[:, 1, :], bank0[:, 2, :]
+        add_terms(gap_sum[1], quarters(1, "win"), closes=False)
+        win0 = piece(1, "win", 0)[:, 0:P]
+        nc.scalar.copy(win0, win_sum[0])
+        win_sum[0] = win0
+        last = piece(1, "win", 1)
+        vector_lose(3, PIECE, PIECE, last)
+        fold(3, "lose", 0, piece(3, "lose", 0), False)
+        fold(1, "lose", 0, piece(1, "lose", 0), True)
+        fold(3, "lose", per_piece, last, False)
+        fold(1, "lose", per_piece, piece(1, "lose", 1), True)
+        add_terms(gap_sum[3], quarters(3, "lose"))
+        add_terms(gap_sum[1], quarters(1, "lose"), opens=False)
+
+        row_sum = keep.tile([P, BLOCKS], F32, name="row_sum")
+        ln_in = keep.tile([P, BLOCKS + V], F32, name="ln_in")
+        ln_out = keep.tile([P, BLOCKS + V], F32, name="ln_out")
+        for b in range(BLOCKS):
+            nc.scalar.activation(piece(0, "win", b % 2), lifted[b][:, 0:S], ACT.Exp, bias=neg_top[:, b : b + 1], accum_out=row_sum[:, b : b + 1])
+        nc.gpsimd.tensor_scalar(ln_in[:, 0:BLOCKS], row_sum[:], 1.0, -1.0, ALU.mult, ALU.add)
+
+        gap_sum[0] = piece(1, "lose", 1)[:, 0:P]
+        nc.vector.scalar_tensor_tensor(gap_sum[0], lose_sum0, -1.0, win0, ALU.mult, ALU.add)
+
+        capped = piece(1, "lose", 0).rearrange("p (n g) -> p n g", g=P)
+        excess = piece(3, "lose", 1).rearrange("p (n g) -> p n g", g=P)
+        linear = keep.tile([P, BLOCKS, P], F32, name="linear")
+        cap = CAP - MARGIN
+
+        for b in (2, 0, 3, 1):
+            nc.vector.tensor_scalar(capped[:, b, :], gap_sum[b], slope, cap, ALU.mult, ALU.min)
+        nc.scalar.activation(ln_in[:, BLOCKS : BLOCKS + V], piece(1, "lose", 0), ACT.Exp, bias=margin[:])
+
+        def take_excess(b):
+            nc.vector.scalar_tensor_tensor(excess[:, b, :], gap_sum[b], slope, capped[:, b, :], ALU.mult, ALU.subtract)
+
+        take_excess(1)
+        add_terms(win_sum[1], quarters(1, "win"))
+        fold(3, "win", 0, picked[3, "win"], False)
+        add_terms(win_sum[3], quarters(3, "win"))
+        for b in (2, 0, 3):
+            take_excess(b)
+        back = {}
+        for b in (2, 0, 1, 3):
+            sign = 1.0 if b in SCALAR_BLOCKS else -1.0
+            nc.vector.scalar_tensor_tensor(linear[:, b, :], win_sum[b], sign * NLL / D, excess[:, b, :], ALU.mult, ALU.add)
+            back[b] = psum.tile([P, G], F32, name=f"back{b}", tag=f"bank{(1, 2, 3, 6)[b]}")
+            nc.tensor.matmul(back[b][:], linear[:, b, :], ident[:], start=True, stop=False, is_transpose=True)
+
+        row_bias = keep.tile([P, BLOCKS], F32, name="row_bias")
+        result = keep.tile([P, BLOCKS, G], F32, name="result")
+        for b in range(BLOCKS):
+            cols = slice(BLOCKS + b * P, BLOCKS + (b + 1) * P)
+            with_sums = slice(0 if b == 0 else cols.start, cols.stop)
+            nc.scalar.activation(ln_out[:, with_sums], ln_in[:, with_sums], ACT.Ln, bias=one)
+            if b == 0:
+                nc.vector.scalar_tensor_tensor(row_bias[:], ln_out[:, 0:BLOCKS], NLL, row_part[:], ALU.mult, ALU.add)
+            nc.tensor.matmul(back[b][:], ln_out[:, cols], ident[:], start=False, stop=True, is_transpose=True)
+            nc.vector.tensor_scalar(result[:, b, :], back[b][:], row_bias[:, b : b + 1], None, ALU.add)
             nc.sync.dma_start(out[b * P : (b + 1) * P, :], result[:, b, :])

@@ -43,16 +43,16 @@ def tile_picked_ysimpo_simpo_p_kernel(tc, x_words, x_scales, hT, offs, win, lose
         h_raw = [keep.tile([P, PACK, P], F32, name=f"h_raw{b}", tag=f"h_raw{b}") for b in range(BLOCKS)]
         h_rows = hT.rearrange("(p j) t -> p j t", j=PACK)
 
+        nc.gpsimd.memset(scales[:].bitcast(I32), 0)
         nc.sync.dma_start(offs_t[:], offs)
+        nc.sync.dma_start(win_t[:], win)
         for q in range(4):
             rows = x_scales[0, 4 * q : 4 * q + 4, :].bitcast(I32)
-            queue = nc.sync if q == 0 else nc.scalar
-            queue.dma_start(scales[32 * q : 32 * q + 32, :].bitcast(I32), rows.unsqueeze(0).to_broadcast([8, 4, T // 4]))
+            nc.scalar.dma_start(scales[32 * q : 32 * q + 4, :].bitcast(I32), rows)
         nc.sync.dma_start(h_raw[0][:], h_rows[:, :, 0:P])
         nc.sync.dma_start(words[:], x_words[0].rearrange("p n t -> p (n t)").bitcast(I32))
         for b in range(1, BLOCKS):
             nc.sync.dma_start(h_raw[b][:], h_rows[:, :, b * P : (b + 1) * P])
-        nc.sync.dma_start(win_t[:], win)
         nc.sync.dma_start(lose_t[:], lose)
         h_block = [h_raw[b][:] for b in range(BLOCKS)]
 
@@ -156,29 +156,15 @@ def tile_picked_ysimpo_simpo_p_kernel(tc, x_words, x_scales, hT, offs, win, lose
             groups = picked[b, name].rearrange("p (g d) -> p g d", d=D)
             return [groups[:, :, d] for d in range(D)]
 
-        halves = {}
-
-        def fold(b, name, first, src, negate):
-            if (b, name) not in halves:
-                slot = "half_late" if (b, name) in ((1, "lose"), (3, "win")) else f"half_{name}{b}"
-                halves[b, name] = keep.tile([P, D // 2, G], F32, name=f"half_{name}{b}", tag=slot)
-            groups = src.rearrange("p (g d) -> p g d", d=D)
-            dst = halves[b, name][:, :, first : first + groups.shape[1]].rearrange("p d g -> p g d")
-            if negate:
-                nc.vector.scalar_tensor_tensor(dst, groups[:, :, 0 : D // 2], -1.0, groups[:, :, D // 2 : D], ALU.mult, ALU.subtract)
-            else:
-                nc.vector.tensor_tensor(dst, groups[:, :, 0 : D // 2], groups[:, :, D // 2 : D], ALU.add)
-
-        def quarters(b, name):
-            return [halves[b, name][:, d, :] for d in range(D // 2)]
+        def add_groups(dst, src):
+            nc.vector.tensor_reduce(dst, src.rearrange("p (g d) -> p g d", d=D), mybir.AxisListType.X, ALU.add)
 
         bank4 = psum.tile([P, P], F32, name="sum_a", tag="bank4")
         bank5 = psum.tile([P, 2, P], F32, name="sum_b", tag="bank5")
         bank6 = psum.tile([P, P], F32, name="sum_c", tag="bank6")
-        bank7 = psum.tile([P, P], F32, name="sum_d", tag="bank7")
         win_sum = {2: bank4[:], 0: bank5[:, 0, :]}
         lose_sum0 = bank6[:]
-        gap_sum = {2: bank5[:, 1, :], 3: bank7[:]}
+        gap_sum = {2: bank5[:, 1, :]}
 
         vector_win(2)
         scalar_gather(0, "win")
@@ -196,65 +182,80 @@ def tile_picked_ysimpo_simpo_p_kernel(tc, x_words, x_scales, hT, offs, win, lose
         scalar_gather(1, "win")
         vector_lose(3, 0, PIECE, piece(3, "lose", 0))
         scalar_gather(1, "lose")
-        fold(1, "win", 0, picked[1, "win"], False)
-        bank0 = psum.tile([P, 3, P], F32, name="sum_e", tag="bank0")
-        gap_sum[1], win_sum[1], win_sum[3] = bank0[:, 0, :], bank0[:, 1, :], bank0[:, 2, :]
-        add_terms(gap_sum[1], quarters(1, "win"), closes=False)
+        win1 = keep.tile([P, G], F32, name="win1")
+        lose1 = keep.tile([P, G], F32, name="lose1", tag="late")
+        gaps = keep.tile([P, 2, G], F32, name="gaps")
+        win_sum[1], gap_sum[1], gap_sum[3] = win1[:], gaps[:, 0, :], gaps[:, 1, :]
+        add_groups(win_sum[1], picked[1, "win"])
         win0 = piece(1, "win", 0)[:, 0:P]
         nc.scalar.copy(win0, win_sum[0])
         win_sum[0] = win0
         last = piece(1, "win", 1)
         vector_lose(3, PIECE, PIECE, last)
-        fold(3, "lose", 0, piece(3, "lose", 0), False)
-        fold(1, "lose", 0, piece(1, "lose", 0), True)
-        fold(3, "lose", per_piece, last, False)
-        fold(1, "lose", per_piece, piece(1, "lose", 1), True)
-        add_terms(gap_sum[3], quarters(3, "lose"))
-        add_terms(gap_sum[1], quarters(1, "lose"), opens=False)
+        add_groups(gap_sum[3][:, 0:per_piece], piece(3, "lose", 0))
+        add_groups(gap_sum[3][:, per_piece:G], last)
+
+        cap = CAP - MARGIN
+        capped_tg = keep.tile([P, 2, G], F32, name="capped_tg", tag="ln_out")
+        capped_gt = piece(3, "lose", 0).rearrange("p (n t) -> p n t", t=P)
+        capped = {2: capped_gt[:, 0, :], 0: capped_gt[:, 1, :], 1: capped_tg[:, 0, :], 3: capped_tg[:, 1, :]}
+
+        def take_capped(b):
+            nc.vector.tensor_scalar(capped[b], gap_sum[b], slope, cap, ALU.mult, ALU.min)
+
+        gap_sum[0] = last[:, 0:P]
+        turned = psum.tile([P, 2, G], F32, name="turned", tag="bank1")
+        take_capped(2)
+        nc.tensor.transpose(turned[:, 0, :], capped[2], ident[:])
+        nc.vector.scalar_tensor_tensor(gap_sum[0], lose_sum0, -1.0, win0, ALU.mult, ALU.add)
+        add_groups(lose1[:, 0:per_piece], piece(1, "lose", 0))
+        take_capped(0)
+        nc.tensor.transpose(turned[:, 1, :], capped[0], ident[:])
+        add_groups(lose1[:, per_piece:G], piece(1, "lose", 1))
+        take_capped(3)
+        nc.vector.tensor_tensor(gap_sum[1], win_sum[1], lose1[:], ALU.subtract)
+        take_capped(1)
 
         row_sum = keep.tile([P, BLOCKS], F32, name="row_sum")
         ln_in = keep.tile([P, BLOCKS + V], F32, name="ln_in")
-        ln_out = keep.tile([P, BLOCKS + V], F32, name="ln_out")
         for b in range(BLOCKS):
             nc.scalar.activation(piece(0, "win", b % 2), lifted[b][:, 0:S], ACT.Exp, bias=neg_top[:, b : b + 1], accum_out=row_sum[:, b : b + 1])
         nc.gpsimd.tensor_scalar(ln_in[:, 0:BLOCKS], row_sum[:], 1.0, -1.0, ALU.mult, ALU.add)
+        finish = (2, 0, 1, 3)
+        middle = BLOCKS + 2 * G
+        nc.scalar.activation(ln_in[:, BLOCKS:middle], turned[:].rearrange("p n g -> p (n g)"), ACT.Exp, bias=margin[:])
+        nc.scalar.activation(ln_in[:, middle : BLOCKS + V], capped_tg[:].rearrange("p n g -> p (n g)"), ACT.Exp, bias=margin[:])
 
-        gap_sum[0] = piece(1, "lose", 1)[:, 0:P]
-        nc.vector.scalar_tensor_tensor(gap_sum[0], lose_sum0, -1.0, win0, ALU.mult, ALU.add)
+        late = keep.tile([P, 2 * BLOCKS + 1, P], F32, name="late", tag="late")
+        excess = {b: late[:, n, :] for n, b in enumerate(finish)}
+        linear = {b: late[:, BLOCKS + n, :] for n, b in enumerate(finish)}
+        win_sum[3] = late[:, 2 * BLOCKS, :]
 
-        capped = piece(1, "lose", 0).rearrange("p (n g) -> p n g", g=P)
-        excess = piece(3, "lose", 1).rearrange("p (n g) -> p n g", g=P)
-        linear = keep.tile([P, BLOCKS, P], F32, name="linear")
-        cap = CAP - MARGIN
-
-        for b in (2, 0, 3, 1):
-            nc.vector.tensor_scalar(capped[:, b, :], gap_sum[b], slope, cap, ALU.mult, ALU.min)
-        nc.scalar.activation(ln_in[:, BLOCKS : BLOCKS + V], piece(1, "lose", 0), ACT.Exp, bias=margin[:])
-
-        def take_excess(b):
-            nc.vector.scalar_tensor_tensor(excess[:, b, :], gap_sum[b], slope, capped[:, b, :], ALU.mult, ALU.subtract)
-
-        take_excess(1)
-        add_terms(win_sum[1], quarters(1, "win"))
-        fold(3, "win", 0, picked[3, "win"], False)
-        add_terms(win_sum[3], quarters(3, "win"))
-        for b in (2, 0, 3):
-            take_excess(b)
-        back = {}
-        for b in (2, 0, 1, 3):
+        def take_linear(b):
             sign = 1.0 if b in SCALAR_BLOCKS else -1.0
-            nc.vector.scalar_tensor_tensor(linear[:, b, :], win_sum[b], sign * NLL / D, excess[:, b, :], ALU.mult, ALU.add)
-            back[b] = psum.tile([P, G], F32, name=f"back{b}", tag=f"bank{(1, 2, 3, 6)[b]}")
-            nc.tensor.matmul(back[b][:], linear[:, b, :], ident[:], start=True, stop=False, is_transpose=True)
+            nc.vector.scalar_tensor_tensor(linear[b], win_sum[b], sign * NLL / D, excess[b], ALU.mult, ALU.add)
 
+        for b in (2, 0):
+            nc.vector.scalar_tensor_tensor(excess[b], gap_sum[b], slope, capped[b], ALU.mult, ALU.subtract)
+        for b in (2, 0):
+            take_linear(b)
+            back = psum.tile([P, G], F32, name=f"back{b}", tag=f"bank{2 + b // 2}")
+            nc.tensor.transpose(back[:], linear[b], ident[:])
+            linear[b] = back[:]
+        nc.vector.scalar_tensor_tensor(late[:, 2:4, :], gaps[:], slope, capped_tg[:], ALU.mult, ALU.subtract)
+        add_groups(win_sum[3], picked[3, "win"])
+        take_linear(1)
+        take_linear(3)
+
+        ln_out = keep.tile([P, BLOCKS + V], F32, name="ln_out", tag="ln_out")
         row_bias = keep.tile([P, BLOCKS], F32, name="row_bias")
         result = keep.tile([P, BLOCKS, G], F32, name="result")
-        for b in range(BLOCKS):
-            cols = slice(BLOCKS + b * P, BLOCKS + (b + 1) * P)
-            with_sums = slice(0 if b == 0 else cols.start, cols.stop)
-            nc.scalar.activation(ln_out[:, with_sums], ln_in[:, with_sums], ACT.Ln, bias=one)
-            if b == 0:
+        for n, b in enumerate(finish):
+            cols = slice(BLOCKS + n * G, BLOCKS + (n + 1) * G)
+            if n == 0:
+                nc.scalar.activation(ln_out[:, 0 : cols.stop], ln_in[:, 0 : cols.stop], ACT.Ln, bias=one)
                 nc.vector.scalar_tensor_tensor(row_bias[:], ln_out[:, 0:BLOCKS], NLL, row_part[:], ALU.mult, ALU.add)
-            nc.tensor.matmul(back[b][:], ln_out[:, cols], ident[:], start=False, stop=True, is_transpose=True)
-            nc.vector.tensor_scalar(result[:, b, :], back[b][:], row_bias[:, b : b + 1], None, ALU.add)
+            else:
+                nc.scalar.activation(ln_out[:, cols], ln_in[:, cols], ACT.Ln, bias=one)
+            nc.vector.scalar_tensor_tensor(result[:, b, :], ln_out[:, cols], row_bias[:, b : b + 1], linear[b], ALU.add, ALU.add)
             nc.sync.dma_start(out[b * P : (b + 1) * P, :], result[:, b, :])

@@ -19,14 +19,15 @@ ACT = mybir.ActivationFunctionType
 
 P = 128
 PACK = 4
+STRIPE = 16
 BLOCKS = V // P
 SCALAR_BLOCKS = (0, 1)
-VECTOR_BLOCKS = (2, 3)
 PIECE = 512
-SCALAR_WINDOW = 2048
-VECTOR_WINDOW = 2048
+WINDOW = 2048
 BETA, MARGIN, NLL = 2.5, 0.7, 0.3
+SLOPE = BETA / D
 CAP = 30.0
+GAP_CAP = CAP - MARGIN
 
 
 def tile_picked_ysimpo_simpo_p_kernel(tc, x_words, x_scales, hT, offs, win, lose, out):
@@ -35,9 +36,9 @@ def tile_picked_ysimpo_simpo_p_kernel(tc, x_words, x_scales, hT, offs, win, lose
         keep = ctx.enter_context(tc.tile_pool(name="keep", bufs=1))
         psum = ctx.enter_context(tc.psum_pool(name="psum", bufs=1))
 
-        offs_t = keep.tile([P, S // 16], U16, name="offs_t")
-        win_t = keep.tile([P, U // 16], U16, name="win_t")
-        lose_t = keep.tile([P, U // 16], U16, name="lose_t")
+        offs_t = keep.tile([P, S // STRIPE], U16, name="offs_t")
+        win_t = keep.tile([P, U // STRIPE], U16, name="win_t")
+        lose_t = keep.tile([P, U // STRIPE], U16, name="lose_t")
         words = keep.tile([P, T], I32, name="words", align_bytes=64)
         scales = keep.tile([P, T], U8, name="scales", align_bytes=64)
         h_raw = [keep.tile([P, PACK, P], F32, name=f"h_raw{b}", tag=f"h_raw{b}") for b in range(BLOCKS)]
@@ -45,70 +46,70 @@ def tile_picked_ysimpo_simpo_p_kernel(tc, x_words, x_scales, hT, offs, win, lose
 
         nc.gpsimd.memset(scales[:].bitcast(I32), 0)
         nc.sync.dma_start(offs_t[:], offs)
-        nc.sync.dma_start(win_t[:], win)
         for q in range(4):
             rows = x_scales[0, 4 * q : 4 * q + 4, :].bitcast(I32)
-            nc.scalar.dma_start(scales[32 * q : 32 * q + 4, :].bitcast(I32), rows)
-        nc.sync.dma_start(h_raw[0][:], h_rows[:, :, 0:P])
+            queue = nc.sync if q < 2 else nc.scalar
+            queue.dma_start(scales[32 * q : 32 * q + 4, :].bitcast(I32), rows)
         nc.sync.dma_start(words[:], x_words[0].rearrange("p n t -> p (n t)").bitcast(I32))
-        for b in range(1, BLOCKS):
+        for b in range(BLOCKS):
             nc.sync.dma_start(h_raw[b][:], h_rows[:, :, b * P : (b + 1) * P])
+        nc.sync.dma_start(win_t[:], win)
         nc.sync.dma_start(lose_t[:], lose)
-        h_block = [h_raw[b][:] for b in range(BLOCKS)]
 
-        ones = keep.tile([P, 2], F32, name="ones")
-        nc.gpsimd.memset(ones[:], 1.0)
-        one = ones[:, 0:1]
+        one = keep.tile([P, 1], F32, name="one")
+        nc.gpsimd.memset(one[:], 1.0)
         margin = keep.tile([P, 1], F32, name="margin")
-        nc.gpsimd.tensor_scalar(margin[:], one, MARGIN, 0.0, ALU.mult, ALU.add)
-        row_part = keep.tile([P, BLOCKS], F32, name="row_part")
-        nc.gpsimd.tensor_scalar(row_part[:, 0:2], ones[:], -NLL, 0.0, ALU.mult, ALU.add)
+        nc.gpsimd.tensor_scalar(margin[:], one[:], MARGIN, 0.0, ALU.mult, ALU.add)
         ident = keep.tile([P, P], F32, name="ident")
         make_identity(nc, ident[:])
 
         warm = keep.tile([P, 1], F32, name="warm")
-        nc.scalar.activation(warm[:], one, ACT.Ln)
+        nc.scalar.activation(warm[:], one[:], ACT.Ln)
 
         x_codes = keep.tile([P, S], U32, name="x_codes", align_bytes=64)
         x_bytes = keep.tile([P, S], U8, name="x_bytes", align_bytes=64)
         nc.vector.tensor_copy(x_bytes[:], scales[:].indirect(offs_t[:]))
         nc.vector.tensor_copy(x_codes[:], words[:].bitcast(U32).indirect(offs_t[:]))
 
+        grouped = []
+        for b in range(BLOCKS):
+            grouped.append(keep.tile([P, P, PACK], BF16, name=f"grouped{b}", align_bytes=64))
+            nc.scalar.copy(
+                grouped[b][:].rearrange("p (c i) j -> p c j i", i=4),
+                h_raw[b][:].rearrange("p j (c i) -> p c j i", i=4),
+            )
+
         logits = {}
 
-        interleaved = []
-        for b in range(BLOCKS):
-            grouped = keep.tile([P, P, PACK], BF16, name=f"grouped{b}", align_bytes=64)
-            nc.scalar.copy(
-                grouped[:].rearrange("p (c i) j -> p c j i", i=4),
-                h_block[b].rearrange("p j (c i) -> p c j i", i=4),
-            )
-            interleaved.append(grouped)
-
         def multiply(b):
-            grouped = interleaved[b]
             h_codes = keep.tile([P, P], U32, name=f"h_codes{b}", tag="h_codes", bufs=3, align_bytes=64)
             h_bytes = keep.tile([P, P], U8, name=f"h_bytes{b}", tag="h_bytes", bufs=3, align_bytes=64)
-            nc.vector.quantize_mx(out=h_codes[:].bitcast(FP8X4), scales=h_bytes[:], in_=grouped[:].rearrange("p t j -> p (t j)"))
-            logits[b] = psum.tile([P, S], F32, name=f"y{b}", tag=f"bank{b}")
+            nc.vector.quantize_mx(
+                out=h_codes[:].bitcast(FP8X4), scales=h_bytes[:], in_=grouped[b][:].rearrange("p t j -> p (t j)")
+            )
+            logits[b] = psum.tile([P, S], F32, name=f"logits{b}", tag=f"bank{b}")
             nc.tensor.matmul_mx(
-                out=logits[b][:], lhsT=h_codes[:].bitcast(FP8X4), lhsT_scale=h_bytes[:],
-                rhs=x_codes[:].bitcast(FP8X4), rhs_scale=x_bytes[:], start=True, stop=True,
+                out=logits[b][:],
+                lhsT=h_codes[:].bitcast(FP8X4),
+                lhsT_scale=h_bytes[:],
+                rhs=x_codes[:].bitcast(FP8X4),
+                rhs_scale=x_bytes[:],
+                start=True,
+                stop=True,
             )
 
         top0 = keep.tile([P, 1], F32, name="top0")
-        top1 = keep.tile([P, 1], F32, name="top1", tag="first_picked")
-        tops = keep.tile([P, 2], F32, name="tops")
-        top = {0: top0[:], 1: top1[:], 2: tops[:, 0:1], 3: tops[:, 1:2]}
+        top1 = keep.tile([P, 1], F32, name="top1", tag="after_windows")
+        top23 = keep.tile([P, 2], F32, name="top23")
+        top = {0: top0[:], 1: top1[:], 2: top23[:, 0:1], 3: top23[:, 1:2]}
         neg_top = keep.tile([P, BLOCKS], F32, name="neg_top")
-
         lifted, window = {}, {}
 
         def open_block(b):
-            lifted[b] = keep.tile([P, S if b in SCALAR_BLOCKS else VECTOR_WINDOW], F32, name=f"lifted{b}")
+            lifted[b] = keep.tile([P, S if b in SCALAR_BLOCKS else WINDOW], F32, name=f"lifted{b}")
             nc.vector.tensor_scalar(lifted[b][:, 0:S], logits[b][:], 1.0, None, ALU.add, ALU.max, accum_out=top[b])
             if b in SCALAR_BLOCKS:
-                window[b] = keep.tile([P, SCALAR_WINDOW], F32, name=f"log_window{b}", tag=f"h_raw{3 - b}")
+                window[b] = keep.tile([P, WINDOW], F32, name=f"log_window{b}", tag=f"h_raw{BLOCKS - 1 - b}")
                 nc.scalar.activation(window[b][:, 0:S], logits[b][:], ACT.Ln, bias=top[b], scale=-1.0)
                 nc.scalar.mul(neg_top[:, b : b + 1], top[b], -1.0)
             else:
@@ -124,138 +125,129 @@ def tile_picked_ysimpo_simpo_p_kernel(tc, x_words, x_scales, hT, offs, win, lose
 
         picked = {}
         for b in range(BLOCKS):
-            both = keep.tile([P, 2 * U], F32, name=f"picked{b}", tag="first_picked" if b == 0 else f"picked{b}")
+            both = keep.tile([P, 2 * U], F32, name=f"picked{b}", tag="after_windows" if b == 0 else f"picked{b}")
             picked[b, "win"], picked[b, "lose"] = both[:, 0:U], both[:, U : 2 * U]
         lists = {"win": win_t, "lose": lose_t}
-        pieces = U // PIECE
-        per_piece = PIECE // D
-        slope = BETA / D
 
         def piece(b, name, h):
             return picked[b, name][:, h * PIECE : (h + 1) * PIECE]
 
-        def looked_up(b, name, first, count):
-            return window[b][:].indirect(lists[name][:, first // 16 : (first + count) // 16])
-
         def scalar_gather(b, name):
-            for h in range(pieces):
-                nc.scalar.activation(piece(b, name, h), looked_up(b, name, h * PIECE, PIECE), ACT.Exp)
+            for h in range(U // PIECE):
+                offsets = lists[name][:, h * PIECE // STRIPE : (h + 1) * PIECE // STRIPE]
+                nc.scalar.activation(piece(b, name, h), window[b][:].indirect(offsets), ACT.Exp)
 
         def vector_win(b):
-            nc.vector.tensor_copy(picked[b, "win"], looked_up(b, "win", 0, U))
+            nc.vector.tensor_copy(picked[b, "win"], window[b][:].indirect(win_t[:]))
 
-        def vector_lose(b, first, count, dst):
-            nc.vector.tensor_tensor(dst, looked_up(b, "lose", first, count), picked[b, "win"][:, first : first + count], ALU.subtract)
+        def vector_lose_less_win(b):
+            nc.vector.tensor_tensor(picked[b, "lose"], window[b][:].indirect(lose_t[:]), picked[b, "win"], ALU.subtract)
 
-        def add_terms(acc, terms, opens=True, closes=True):
-            for i, term in enumerate(terms):
-                first, final = opens and i == 0, closes and i == len(terms) - 1
-                nc.tensor.matmul(acc, term, ident[:], start=first, stop=final, is_transpose=True)
-
-        def eighths(b, name):
+        def sum_by_transposes(acc, b, name):
             groups = picked[b, name].rearrange("p (g d) -> p g d", d=D)
-            return [groups[:, :, d] for d in range(D)]
+            for d in range(D):
+                nc.tensor.matmul(acc, groups[:, :, d], ident[:], start=(d == 0), stop=(d == D - 1), is_transpose=True)
 
-        def add_groups(dst, src):
+        def sum_by_reduce(dst, src):
             nc.vector.tensor_reduce(dst, src.rearrange("p (g d) -> p g d", d=D), mybir.AxisListType.X, ALU.add)
 
-        bank4 = psum.tile([P, P], F32, name="sum_a", tag="bank4")
-        bank5 = psum.tile([P, 2, P], F32, name="sum_b", tag="bank5")
-        bank6 = psum.tile([P, P], F32, name="sum_c", tag="bank6")
-        win_sum = {2: bank4[:], 0: bank5[:, 0, :]}
-        lose_sum0 = bank6[:]
-        gap_sum = {2: bank5[:, 1, :]}
+        win2_gt = psum.tile([P, P], F32, name="win2_gt", tag="bank4")
+        shared = psum.tile([P, 2, P], F32, name="shared", tag="bank5")
+        win0_psum, gap2_gt = shared[:, 0, :], shared[:, 1, :]
+        lose0_gt = psum.tile([P, P], F32, name="lose0_gt", tag="bank6")
+        win1_psum = psum.tile([P, P], F32, name="win1_psum", tag="bank7")
 
         vector_win(2)
         scalar_gather(0, "win")
-        add_terms(win_sum[2], eighths(2, "win"))
-        add_terms(win_sum[0], eighths(0, "win"))
-        vector_lose(2, 0, U, picked[2, "lose"])
+        sum_by_transposes(win2_gt[:], 2, "win")
+        sum_by_transposes(win0_psum, 0, "win")
+        vector_lose_less_win(2)
         scalar_gather(0, "lose")
-        add_terms(gap_sum[2], eighths(2, "lose"))
-        add_terms(lose_sum0, eighths(0, "lose"))
+        sum_by_transposes(gap2_gt, 2, "lose")
+        sum_by_transposes(lose0_gt[:], 0, "lose")
         open_block(3)
-        nc.gpsimd.tensor_scalar(neg_top[:, 2:4], tops[:], -1.0, 0.0, ALU.mult, ALU.add)
-        nc.gpsimd.tensor_scalar(row_part[:, 2:4], tops[:], NLL, 0.0, ALU.mult, ALU.add)
-
         vector_win(3)
         scalar_gather(1, "win")
-        vector_lose(3, 0, PIECE, piece(3, "lose", 0))
+        sum_by_transposes(win1_psum[:], 1, "win")
+        vector_lose_less_win(3)
         scalar_gather(1, "lose")
-        win1 = keep.tile([P, G], F32, name="win1")
-        lose1 = keep.tile([P, G], F32, name="lose1", tag="late")
-        gaps = keep.tile([P, 2, G], F32, name="gaps")
-        win_sum[1], gap_sum[1], gap_sum[3] = win1[:], gaps[:, 0, :], gaps[:, 1, :]
-        add_groups(win_sum[1], picked[1, "win"])
-        win0 = piece(1, "win", 0)[:, 0:P]
-        nc.scalar.copy(win0, win_sum[0])
-        win_sum[0] = win0
-        last = piece(1, "win", 1)
-        vector_lose(3, PIECE, PIECE, last)
-        add_groups(gap_sum[3][:, 0:per_piece], piece(3, "lose", 0))
-        add_groups(gap_sum[3][:, per_piece:G], last)
 
-        cap = CAP - MARGIN
-        capped_tg = keep.tile([P, 2, G], F32, name="capped_tg", tag="ln_out")
-        capped_gt = piece(3, "lose", 0).rearrange("p (n t) -> p n t", t=P)
-        capped = {2: capped_gt[:, 0, :], 0: capped_gt[:, 1, :], 1: capped_tg[:, 0, :], 3: capped_tg[:, 1, :]}
+        lose1_tg = keep.tile([P, G], F32, name="lose1_tg", tag="after_gaps")
+        gap13_tg = keep.tile([P, 2, G], F32, name="gap13_tg")
+        sum_by_reduce(gap13_tg[:, 1, :], picked[3, "lose"])
 
-        def take_capped(b):
-            nc.vector.tensor_scalar(capped[b], gap_sum[b], slope, cap, ALU.mult, ALU.min)
-
-        gap_sum[0] = last[:, 0:P]
-        turned = psum.tile([P, 2, G], F32, name="turned", tag="bank1")
-        take_capped(2)
-        nc.tensor.transpose(turned[:, 0, :], capped[2], ident[:])
-        nc.vector.scalar_tensor_tensor(gap_sum[0], lose_sum0, -1.0, win0, ALU.mult, ALU.add)
-        add_groups(lose1[:, 0:per_piece], piece(1, "lose", 0))
-        take_capped(0)
-        nc.tensor.transpose(turned[:, 1, :], capped[0], ident[:])
-        add_groups(lose1[:, per_piece:G], piece(1, "lose", 1))
-        take_capped(3)
-        nc.vector.tensor_tensor(gap_sum[1], win_sum[1], lose1[:], ALU.subtract)
-        take_capped(1)
-
+        win01_gt = keep.tile([P, 2, P], F32, name="win01_gt")
+        nc.scalar.copy(win01_gt[:, 0, :], win0_psum)
+        nc.scalar.mul(neg_top[:, 2:4], top23[:], -1.0)
         row_sum = keep.tile([P, BLOCKS], F32, name="row_sum")
-        ln_in = keep.tile([P, BLOCKS + V], F32, name="ln_in")
+        win1_tg = psum.tile([P, G], F32, name="win1_tg", tag="bank0")
         for b in range(BLOCKS):
-            nc.scalar.activation(piece(0, "win", b % 2), lifted[b][:, 0:S], ACT.Exp, bias=neg_top[:, b : b + 1], accum_out=row_sum[:, b : b + 1])
-        nc.gpsimd.tensor_scalar(ln_in[:, 0:BLOCKS], row_sum[:], 1.0, -1.0, ALU.mult, ALU.add)
+            if b == BLOCKS // 2:
+                nc.scalar.copy(win01_gt[:, 1, :], win1_psum[:])
+                nc.tensor.transpose(win1_tg[:], win01_gt[:, 1, :], ident[:])
+            nc.scalar.activation(
+                piece(0, "win", b % 2),
+                lifted[b][:, 0:S],
+                ACT.Exp,
+                bias=neg_top[:, b : b + 1],
+                accum_out=row_sum[:, b : b + 1],
+            )
+
+        capped13_tg = keep.tile([P, 2, G], F32, name="capped13_tg", tag="after_exp")
+        capped20_gt = keep.tile([P, 2, P], F32, name="capped20_gt")
+        capped20_tg = psum.tile([P, 2, G], F32, name="capped20_tg", tag="bank1")
+        gap0_gt = keep.tile([P, P], F32, name="gap0_gt")
+
+        def cap_and_turn(n, gap_gt):
+            nc.vector.tensor_scalar(capped20_gt[:, n, :], gap_gt, SLOPE, GAP_CAP, ALU.mult, ALU.min)
+            nc.tensor.transpose(capped20_tg[:, n, :], capped20_gt[:, n, :], ident[:])
+
+        half = G // 2
+        cap_and_turn(0, gap2_gt)
+        sum_by_reduce(lose1_tg[:, 0:half], piece(1, "lose", 0))
+        nc.vector.scalar_tensor_tensor(gap0_gt[:], lose0_gt[:], -1.0, win01_gt[:, 0, :], ALU.mult, ALU.add)
+        sum_by_reduce(lose1_tg[:, half:G], piece(1, "lose", 1))
+        cap_and_turn(1, gap0_gt[:])
+        nc.vector.scalar_tensor_tensor(gap13_tg[:, 0, :], lose1_tg[:], -1.0, win1_tg[:], ALU.mult, ALU.add)
+        nc.vector.tensor_scalar(capped13_tg[:], gap13_tg[:], SLOPE, GAP_CAP, ALU.mult, ALU.min)
+
         finish = (2, 0, 1, 3)
-        middle = BLOCKS + 2 * G
-        nc.scalar.activation(ln_in[:, BLOCKS:middle], turned[:].rearrange("p n g -> p (n g)"), ACT.Exp, bias=margin[:])
-        nc.scalar.activation(ln_in[:, middle : BLOCKS + V], capped_tg[:].rearrange("p n g -> p (n g)"), ACT.Exp, bias=margin[:])
+        exps = keep.tile([P, BLOCKS, G], F32, name="exps")
+        nc.scalar.activation(exps[:, 0:2, :], capped20_tg[:], ACT.Exp, bias=margin[:])
+        nc.scalar.activation(exps[:, 2:4, :], capped13_tg[:], ACT.Exp, bias=margin[:])
 
-        late = keep.tile([P, 2 * BLOCKS + 1, P], F32, name="late", tag="late")
-        excess = {b: late[:, n, :] for n, b in enumerate(finish)}
-        linear = {b: late[:, BLOCKS + n, :] for n, b in enumerate(finish)}
-        win_sum[3] = late[:, 2 * BLOCKS, :]
+        late = keep.tile([P, 2 * BLOCKS + 1, P], F32, name="late", tag="after_gaps")
+        above = [late[:, n, :] for n in range(BLOCKS)]
+        linear = [late[:, BLOCKS + n, :] for n in range(BLOCKS)]
+        row_part = late[:, 2 * BLOCKS, 0:BLOCKS]
+        win3_tg = above[1]
+        win_sum = [win2_gt[:], win01_gt[:, 0, :], win1_tg[:], win3_tg]
 
-        def take_linear(b):
-            sign = 1.0 if b in SCALAR_BLOCKS else -1.0
-            nc.vector.scalar_tensor_tensor(linear[b], win_sum[b], sign * NLL / D, excess[b], ALU.mult, ALU.add)
+        def take_linear(n):
+            sign = 1.0 if finish[n] in SCALAR_BLOCKS else -1.0
+            nc.vector.scalar_tensor_tensor(linear[n], win_sum[n], sign * NLL / D, above[n], ALU.mult, ALU.add)
 
-        for b in (2, 0):
-            nc.vector.scalar_tensor_tensor(excess[b], gap_sum[b], slope, capped[b], ALU.mult, ALU.subtract)
-        for b in (2, 0):
-            take_linear(b)
-            back = psum.tile([P, G], F32, name=f"back{b}", tag=f"bank{2 + b // 2}")
-            nc.tensor.transpose(back[:], linear[b], ident[:])
-            linear[b] = back[:]
-        nc.vector.scalar_tensor_tensor(late[:, 2:4, :], gaps[:], slope, capped_tg[:], ALU.mult, ALU.subtract)
-        add_groups(win_sum[3], picked[3, "win"])
-        take_linear(1)
+        for n, gap_gt in enumerate((gap2_gt, gap0_gt[:])):
+            nc.vector.tensor_scalar(above[n], gap_gt, SLOPE, GAP_CAP, ALU.mult, ALU.max)
+        nc.vector.tensor_scalar(late[:, 2:4, :], gap13_tg[:], SLOPE, GAP_CAP, ALU.mult, ALU.max)
+        for n in range(2):
+            take_linear(n)
+            turned = psum.tile([P, G], F32, name=f"linear_tg{n}", tag=f"bank{2 + n}")
+            nc.tensor.transpose(turned[:], linear[n], ident[:])
+            linear[n] = turned[:]
+        nc.vector.tensor_scalar(row_part[:, 0:2], one[:].to_broadcast([P, 2]), -NLL, -GAP_CAP, ALU.mult, ALU.add)
+        nc.vector.tensor_scalar(row_part[:, 2:4], top23[:], NLL, -GAP_CAP, ALU.mult, ALU.add)
+        take_linear(2)
+        sum_by_reduce(win3_tg, picked[3, "win"])
         take_linear(3)
 
-        ln_out = keep.tile([P, BLOCKS + V], F32, name="ln_out", tag="ln_out")
+        logs = keep.tile([P, BLOCKS + 1, G], F32, name="logs", tag="after_exp")
+        log_sum = logs[:, BLOCKS, 0:BLOCKS]
         row_bias = keep.tile([P, BLOCKS], F32, name="row_bias")
         result = keep.tile([P, BLOCKS, G], F32, name="result")
+        nc.scalar.activation(log_sum, row_sum[:], ACT.Ln)
+        nc.vector.scalar_tensor_tensor(row_bias[:], log_sum, NLL, row_part, ALU.mult, ALU.add)
         for n, b in enumerate(finish):
-            cols = slice(BLOCKS + n * G, BLOCKS + (n + 1) * G)
-            if n == 0:
-                nc.scalar.activation(ln_out[:, 0 : cols.stop], ln_in[:, 0 : cols.stop], ACT.Ln, bias=one)
-                nc.vector.scalar_tensor_tensor(row_bias[:], ln_out[:, 0:BLOCKS], NLL, row_part[:], ALU.mult, ALU.add)
-            else:
-                nc.scalar.activation(ln_out[:, cols], ln_in[:, cols], ACT.Ln, bias=one)
-            nc.vector.scalar_tensor_tensor(result[:, b, :], ln_out[:, cols], row_bias[:, b : b + 1], linear[b], ALU.add, ALU.add)
-            nc.sync.dma_start(out[b * P : (b + 1) * P, :], result[:, b, :])
+            nc.scalar.activation(logs[:, n, :], exps[:, n, :], ACT.Ln, bias=one[:])
+            nc.vector.scalar_tensor_tensor(result[:, n, :], logs[:, n, :], row_bias[:, b : b + 1], linear[n], ALU.add, ALU.add)
+            nc.sync.dma_start(out[b * P : (b + 1) * P, :], result[:, n, :])

from contextlib import ExitStack

import concourse.mybir as mybir
from concourse.masks import make_identity

K, T, S, V, D, U = 512, 1024, 512, 512, 8, 1024
G = U // D
FLOPS = 2 * K * V * S

F32 = mybir.dt.float32
BF16 = mybir.dt.bfloat16
I32 = mybir.dt.int32
U32 = mybir.dt.uint32
U16 = mybir.dt.uint16
U8 = mybir.dt.uint8
FP8X4 = mybir.dt.float8_e4m3fn_x4
ALU = mybir.AluOpType
ACT = mybir.ActivationFunctionType

P = 128
PACK = 4
STRIPE = 16
BLOCKS = V // P
SCALAR_BLOCKS = (0, 1)
PIECE = 512
WINDOW = 2048
BETA, MARGIN, NLL = 2.5, 0.7, 0.3
SLOPE = BETA / D
CAP = 30.0
GAP_CAP = CAP - MARGIN


def tile_picked_ysimpo_simpo_p_kernel(tc, x_words, x_scales, hT, offs, win, lose, out):
    nc = tc.nc
    with ExitStack() as ctx:
        keep = ctx.enter_context(tc.tile_pool(name="keep", bufs=1))
        psum = ctx.enter_context(tc.psum_pool(name="psum", bufs=1))

        offs_t = keep.tile([P, S // STRIPE], U16, name="offs_t")
        win_t = keep.tile([P, U // STRIPE], U16, name="win_t")
        lose_t = keep.tile([P, U // STRIPE], U16, name="lose_t")
        words = keep.tile([P, T], I32, name="words", align_bytes=64)
        scales = keep.tile([P, T], U8, name="scales", align_bytes=64)
        h_raw = [keep.tile([P, PACK, P], F32, name=f"h_raw{b}", tag=f"h_raw{b}") for b in range(BLOCKS)]
        h_rows = hT.rearrange("(p j) t -> p j t", j=PACK)

        nc.gpsimd.memset(scales[:].bitcast(I32), 0)
        nc.sync.dma_start(offs_t[:], offs)
        for q in range(4):
            rows = x_scales[0, 4 * q : 4 * q + 4, :].bitcast(I32)
            queue = nc.sync if q < 2 else nc.scalar
            queue.dma_start(scales[32 * q : 32 * q + 4, :].bitcast(I32), rows)
        nc.sync.dma_start(words[:], x_words[0].rearrange("p n t -> p (n t)").bitcast(I32))
        for b in range(BLOCKS):
            nc.sync.dma_start(h_raw[b][:], h_rows[:, :, b * P : (b + 1) * P])
        nc.sync.dma_start(win_t[:], win)
        nc.sync.dma_start(lose_t[:], lose)

        one = keep.tile([P, 1], F32, name="one")
        nc.gpsimd.memset(one[:], 1.0)
        margin = keep.tile([P, 1], F32, name="margin")
        nc.gpsimd.tensor_scalar(margin[:], one[:], MARGIN, 0.0, ALU.mult, ALU.add)
        ident = keep.tile([P, P], F32, name="ident")
        make_identity(nc, ident[:])

        warm = keep.tile([P, 1], F32, name="warm")
        nc.scalar.activation(warm[:], one[:], ACT.Ln)

        x_codes = keep.tile([P, S], U32, name="x_codes", align_bytes=64)
        x_bytes = keep.tile([P, S], U8, name="x_bytes", align_bytes=64)
        nc.vector.tensor_copy(x_bytes[:], scales[:].indirect(offs_t[:]))
        nc.vector.tensor_copy(x_codes[:], words[:].bitcast(U32).indirect(offs_t[:]))

        grouped = []
        for b in range(BLOCKS):
            grouped.append(keep.tile([P, P, PACK], BF16, name=f"grouped{b}", align_bytes=64))
            nc.scalar.copy(
                grouped[b][:].rearrange("p (c i) j -> p c j i", i=4),
                h_raw[b][:].rearrange("p j (c i) -> p c j i", i=4),
            )

        logits = {}

        def multiply(b):
            h_codes = keep.tile([P, P], U32, name=f"h_codes{b}", tag="h_codes", bufs=3, align_bytes=64)
            h_bytes = keep.tile([P, P], U8, name=f"h_bytes{b}", tag="h_bytes", bufs=3, align_bytes=64)
            nc.vector.quantize_mx(
                out=h_codes[:].bitcast(FP8X4), scales=h_bytes[:], in_=grouped[b][:].rearrange("p t j -> p (t j)")
            )
            logits[b] = psum.tile([P, S], F32, name=f"logits{b}", tag=f"bank{b}")
            nc.tensor.matmul_mx(
                out=logits[b][:],
                lhsT=h_codes[:].bitcast(FP8X4),
                lhsT_scale=h_bytes[:],
                rhs=x_codes[:].bitcast(FP8X4),
                rhs_scale=x_bytes[:],
                start=True,
                stop=True,
            )

        top0 = keep.tile([P, 1], F32, name="top0")
        top1 = keep.tile([P, 1], F32, name="top1", tag="after_windows")
        top23 = keep.tile([P, 2], F32, name="top23")
        top = {0: top0[:], 1: top1[:], 2: top23[:, 0:1], 3: top23[:, 1:2]}
        neg_top = keep.tile([P, BLOCKS], F32, name="neg_top")
        lifted, window = {}, {}

        def open_block(b):
            lifted[b] = keep.tile([P, S if b in SCALAR_BLOCKS else WINDOW], F32, name=f"lifted{b}")
            nc.vector.tensor_scalar(lifted[b][:, 0:S], logits[b][:], 1.0, None, ALU.add, ALU.max, accum_out=top[b])
            if b in SCALAR_BLOCKS:
                window[b] = keep.tile([P, WINDOW], F32, name=f"log_window{b}", tag=f"h_raw{BLOCKS - 1 - b}")
                nc.scalar.activation(window[b][:, 0:S], logits[b][:], ACT.Ln, bias=top[b], scale=-1.0)
                nc.scalar.mul(neg_top[:, b : b + 1], top[b], -1.0)
            else:
                window[b] = lifted[b]

        multiply(0)
        multiply(1)
        multiply(2)
        open_block(0)
        open_block(1)
        open_block(2)
        multiply(3)

        picked = {}
        for b in range(BLOCKS):
            both = keep.tile([P, 2 * U], F32, name=f"picked{b}", tag="after_windows" if b == 0 else f"picked{b}")
            picked[b, "win"], picked[b, "lose"] = both[:, 0:U], both[:, U : 2 * U]
        lists = {"win": win_t, "lose": lose_t}

        def piece(b, name, h):
            return picked[b, name][:, h * PIECE : (h + 1) * PIECE]

        def scalar_gather(b, name):
            for h in range(U // PIECE):
                offsets = lists[name][:, h * PIECE // STRIPE : (h + 1) * PIECE // STRIPE]
                nc.scalar.activation(piece(b, name, h), window[b][:].indirect(offsets), ACT.Exp)

        def vector_win(b):
            nc.vector.tensor_copy(picked[b, "win"], window[b][:].indirect(win_t[:]))

        def vector_lose_less_win(b):
            nc.vector.tensor_tensor(picked[b, "lose"], window[b][:].indirect(lose_t[:]), picked[b, "win"], ALU.subtract)

        def sum_by_transposes(acc, b, name):
            groups = picked[b, name].rearrange("p (g d) -> p g d", d=D)
            for d in range(D):
                nc.tensor.matmul(acc, groups[:, :, d], ident[:], start=(d == 0), stop=(d == D - 1), is_transpose=True)

        def sum_by_reduce(dst, src):
            nc.vector.tensor_reduce(dst, src.rearrange("p (g d) -> p g d", d=D), mybir.AxisListType.X, ALU.add)

        win2_gt = psum.tile([P, P], F32, name="win2_gt", tag="bank4")
        shared = psum.tile([P, 2, P], F32, name="shared", tag="bank5")
        win0_psum, gap2_gt = shared[:, 0, :], shared[:, 1, :]
        lose0_gt = psum.tile([P, P], F32, name="lose0_gt", tag="bank6")
        win1_psum = psum.tile([P, P], F32, name="win1_psum", tag="bank7")

        vector_win(2)
        scalar_gather(0, "win")
        sum_by_transposes(win2_gt[:], 2, "win")
        sum_by_transposes(win0_psum, 0, "win")
        vector_lose_less_win(2)
        scalar_gather(0, "lose")
        sum_by_transposes(gap2_gt, 2, "lose")
        sum_by_transposes(lose0_gt[:], 0, "lose")
        open_block(3)
        vector_win(3)
        scalar_gather(1, "win")
        sum_by_transposes(win1_psum[:], 1, "win")
        vector_lose_less_win(3)
        scalar_gather(1, "lose")

        lose1_tg = keep.tile([P, G], F32, name="lose1_tg", tag="after_gaps")
        gap13_tg = keep.tile([P, 2, G], F32, name="gap13_tg")
        sum_by_reduce(gap13_tg[:, 1, :], picked[3, "lose"])

        win01_gt = keep.tile([P, 2, P], F32, name="win01_gt")
        nc.scalar.copy(win01_gt[:, 0, :], win0_psum)
        nc.scalar.mul(neg_top[:, 2:4], top23[:], -1.0)
        row_sum = keep.tile([P, BLOCKS], F32, name="row_sum")
        win1_tg = psum.tile([P, G], F32, name="win1_tg", tag="bank0")
        for b in range(BLOCKS):
            if b == BLOCKS // 2:
                nc.scalar.copy(win01_gt[:, 1, :], win1_psum[:])
                nc.tensor.transpose(win1_tg[:], win01_gt[:, 1, :], ident[:])
            nc.scalar.activation(
                piece(0, "win", b % 2),
                lifted[b][:, 0:S],
                ACT.Exp,
                bias=neg_top[:, b : b + 1],
                accum_out=row_sum[:, b : b + 1],
            )

        capped13_tg = keep.tile([P, 2, G], F32, name="capped13_tg", tag="after_exp")
        capped20_gt = keep.tile([P, 2, P], F32, name="capped20_gt")
        capped20_tg = psum.tile([P, 2, G], F32, name="capped20_tg", tag="bank1")
        gap0_gt = keep.tile([P, P], F32, name="gap0_gt")

        def cap_and_turn(n, gap_gt):
            nc.vector.tensor_scalar(capped20_gt[:, n, :], gap_gt, SLOPE, GAP_CAP, ALU.mult, ALU.min)
            nc.tensor.transpose(capped20_tg[:, n, :], capped20_gt[:, n, :], ident[:])

        half = G // 2
        cap_and_turn(0, gap2_gt)
        sum_by_reduce(lose1_tg[:, 0:half], piece(1, "lose", 0))
        nc.vector.scalar_tensor_tensor(gap0_gt[:], lose0_gt[:], -1.0, win01_gt[:, 0, :], ALU.mult, ALU.add)
        sum_by_reduce(lose1_tg[:, half:G], piece(1, "lose", 1))
        cap_and_turn(1, gap0_gt[:])
        nc.vector.scalar_tensor_tensor(gap13_tg[:, 0, :], lose1_tg[:], -1.0, win1_tg[:], ALU.mult, ALU.add)
        nc.vector.tensor_scalar(capped13_tg[:], gap13_tg[:], SLOPE, GAP_CAP, ALU.mult, ALU.min)

        finish = (2, 0, 1, 3)
        exps = keep.tile([P, BLOCKS, G], F32, name="exps")
        nc.scalar.activation(exps[:, 0:2, :], capped20_tg[:], ACT.Exp, bias=margin[:])
        nc.scalar.activation(exps[:, 2:4, :], capped13_tg[:], ACT.Exp, bias=margin[:])

        late = keep.tile([P, 2 * BLOCKS + 1, P], F32, name="late", tag="after_gaps")
        above = [late[:, n, :] for n in range(BLOCKS)]
        linear = [late[:, BLOCKS + n, :] for n in range(BLOCKS)]
        row_part = late[:, 2 * BLOCKS, 0:BLOCKS]
        win3_tg = above[1]
        win_sum = [win2_gt[:], win01_gt[:, 0, :], win1_tg[:], win3_tg]

        def take_linear(n):
            sign = 1.0 if finish[n] in SCALAR_BLOCKS else -1.0
            nc.vector.scalar_tensor_tensor(linear[n], win_sum[n], sign * NLL / D, above[n], ALU.mult, ALU.add)

        for n, gap_gt in enumerate((gap2_gt, gap0_gt[:])):
            nc.vector.tensor_scalar(above[n], gap_gt, SLOPE, GAP_CAP, ALU.mult, ALU.max)
        nc.vector.tensor_scalar(late[:, 2:4, :], gap13_tg[:], SLOPE, GAP_CAP, ALU.mult, ALU.max)
        for n in range(2):
            take_linear(n)
            turned = psum.tile([P, G], F32, name=f"linear_tg{n}", tag=f"bank{2 + n}")
            nc.tensor.transpose(turned[:], linear[n], ident[:])
            linear[n] = turned[:]
        nc.vector.tensor_scalar(row_part[:, 0:2], one[:].to_broadcast([P, 2]), -NLL, -GAP_CAP, ALU.mult, ALU.add)
        nc.vector.tensor_scalar(row_part[:, 2:4], top23[:], NLL, -GAP_CAP, ALU.mult, ALU.add)
        take_linear(2)
        sum_by_reduce(win3_tg, picked[3, "win"])
        take_linear(3)

        logs = keep.tile([P, BLOCKS + 1, G], F32, name="logs", tag="after_exp")
        log_sum = logs[:, BLOCKS, 0:BLOCKS]
        row_bias = keep.tile([P, BLOCKS], F32, name="row_bias")
        result = keep.tile([P, BLOCKS, G], F32, name="result")
        nc.scalar.activation(log_sum, row_sum[:], ACT.Ln)
        nc.vector.scalar_tensor_tensor(row_bias[:], log_sum, NLL, row_part, ALU.mult, ALU.add)
        for n, b in enumerate(finish):
            nc.scalar.activation(logs[:, n, :], exps[:, n, :], ACT.Ln, bias=one[:])
            nc.vector.scalar_tensor_tensor(result[:, n, :], logs[:, n, :], row_bias[:, b : b + 1], linear[n], ALU.add, ALU.add)
            nc.sync.dma_start(out[b * P : (b + 1) * P, :], result[:, n, :])
